import numpy as np
import ml_dtypes


def mxq(x, axis, fmt="e4m3"):
    dtype, down = {"e4m3": (ml_dtypes.float8_e4m3fn, 7), "e5m2": (ml_dtypes.float8_e5m2, 14)}[fmt]
    v = np.moveaxis(np.asarray(x, np.float32).astype(ml_dtypes.bfloat16).astype(np.float64), axis, -1)
    blocks = v.reshape(v.shape[:-1] + (-1, 32))
    amax = np.abs(blocks).max(-1, keepdims=True)
    byte = np.maximum(np.where(amax > 0, np.frexp(amax)[1] - 1 + 127, 0) - down, 1)
    scale = np.exp2(byte - 127.0)
    codes = (blocks / scale).astype(np.float32).astype(dtype).astype(np.float64)
    return np.moveaxis((codes * scale).reshape(v.shape), -1, axis)


WIDE = False


def mx_kscale(k):
    if not WIDE:
        return np.ones(k)
    levels = np.array([10, -10, 5, -5, 0])
    if k % 512:
        return np.exp2(np.random.permutation(np.resize(levels, k // 32))).repeat(32)
    a = np.empty((k // 512, 16))
    for p in range(k // 512):
        a[p, :8] = np.random.permutation(np.resize(levels, 8))
        for g in range(8):
            far = levels[np.abs(levels - a[p, g]) >= 10]
            a[p, g + 8] = far[np.random.randint(len(far))]
    return np.exp2(a.ravel()).repeat(32)


def f64(x):
    return np.asarray(x).astype(np.float64)


def striped(idx):
    return np.tile(np.asarray(idx).reshape(-1, 16).T, (8, 1)).astype(np.uint16)


def unstriped(offs):
    return offs[:16].T.reshape(-1).astype(np.int64)


G, K, T, D, M = 256, 4, 4096, 512, 384


def setup_inputs():
    n = np.random.standard_normal
    s = mx_kscale(D)[:, None]
    grid = lambda x: np.round(x * 32) / 32
    x = grid(n((D, T))) * s
    idx = np.random.randint(0, T, (G, K))
    part = np.random.randint(1, 128 // K, (G, K)) / 64.0
    return {
        "xT": x.astype(np.float32),
        "w": (n((D, M)) / np.sqrt(D) / s).astype(np.float32),
        "part": np.tile(part.reshape(-1), (128, 1)).astype(np.float32),
        "bias": (0.3 * n((M, 1))).astype(np.float32),
        "offs": striped(idx.reshape(-1)),
    }


def reference(xT, w, part, bias, offs):
    x = f64(xT)[:, unstriped(offs)]
    y = mxq(f64(w), 0, "e4m3").T @ mxq((x * f64(part)[:1]).reshape(D, G, K).sum(-1), 0, "e4m3")
    y = y + f64(bias)
    return y

@@ -1,0 +1,136 @@
+from contextlib import ExitStack
+
+import concourse.mybir as mybir
+from concourse.masks import make_identity
+
+G, K, T, D, M = 256, 4, 4096, 512, 384
+FLOPS = 2 * D * M * G
+BYTES = 4 * (D * T + D * M + G * K + M + M * G) + 2 * 128 * (G * K // 16)
+
+F32 = mybir.dt.float32
+BF16 = mybir.dt.bfloat16
+U32 = mybir.dt.uint32
+U16 = mybir.dt.uint16
+U8 = mybir.dt.uint8
+FP8X4 = mybir.dt.float8_e4m3fn_x4
+MULT = mybir.AluOpType.mult
+ADD = mybir.AluOpType.add
+IDENTITY = mybir.ActivationFunctionType.Identity
+
+P = 128
+PACK = 4
+ENTRIES = G * K
+PER_COLUMN = 16
+M_TILES = M // P
+PART_ROW = ENTRIES // P
+POINT_RUNS = ((0, 128), (128, 256))
+W_RUNS = ((0, 256), (256, 384))
+
+
+def tile_attend_grid_bias_kernel(tc, xT, w, part, bias, offs, out):
+    nc = tc.nc
+    with ExitStack() as ctx:
+        keep = ctx.enter_context(tc.tile_pool(name="keep", bufs=1))
+        psum = ctx.enter_context(tc.psum_pool(name="psum", bufs=1))
+
+        offsets = keep.tile([P, ENTRIES // PER_COLUMN], U16, name="offsets")
+        part_rows = keep.tile([P, PART_ROW], F32, name="part_rows")
+        planes = [keep.tile([P, T], F32, name=f"plane{t}") for t in range(PACK)]
+        w_raw = [keep.tile([P, PACK, hi - lo], F32, name=f"w_raw{lo}") for lo, hi in W_RUNS]
+        bias_cols = keep.tile([P, M_TILES], F32, name="bias_cols")
+
+        x_rows = xT.rearrange("(p t) c -> p t c", t=PACK)
+        w_rows = w.rearrange("(p t) m -> p t m", t=PACK)
+        nc.scalar.dma_start(out=part_rows[:], in_=part[0:1, :].rearrange("o (n r) -> (o n) r", r=PART_ROW))
+        nc.sync.dma_start(out=planes[0][:], in_=x_rows[:, 0, :])
+        nc.sync.dma_start(offsets[:], offs)
+        for t in range(1, PACK):
+            nc.sync.dma_start(out=planes[t][:], in_=x_rows[:, t, :])
+        for raw, (lo, hi) in zip(w_raw, W_RUNS):
+            nc.sync.dma_start(out=raw[:], in_=w_rows[:, :, lo:hi])
+        with nc.allow_non_contiguous_dma(reason="one bias value to a partition"):
+            nc.sync.dma_start(out=bias_cols[:], in_=bias.rearrange("(c p) o -> p (c o)", p=P))
+
+        identity = keep.tile([P, P], F32, name="identity")
+        make_identity(nc, identity[:])
+        weights = keep.tile([P, P, PART_ROW], F32, name="weights")
+        for half in range(2):
+            spread = psum.tile([P, 4, P], F32, name=f"spread{half}")
+            for r in range(4):
+                column = part_rows[:, 4 * half + r : 4 * half + r + 1]
+                nc.tensor.transpose(spread[:, r, :], column.to_broadcast([P, P]), identity[:])
+            nc.scalar.copy(out=weights[:, :, 4 * half : 4 * half + 4], in_=spread[:].rearrange("p r n -> p n r"))
+        weights_flat = weights[:].rearrange("p n r -> p (n r)")
+
+        e_grouped = keep.tile([P, G, PACK], BF16, name="e_grouped", align_bytes=64)
+        e_codes = keep.tile([P, G], U32, name="e_codes", align_bytes=64)
+        e_scales = keep.tile([P, G], U8, name="e_scales", align_bytes=64)
+        w_grouped = keep.tile([P, M, PACK], BF16, name="w_grouped", align_bytes=64)
+        w_codes = keep.tile([P, M], U32, name="w_codes", align_bytes=64)
+        w_scales = keep.tile([P, M], U8, name="w_scales", align_bytes=64)
+
+        def gather(t, lo, hi):
+            products = keep.tile([P, (hi - lo) * K], F32, name=f"products{t}_{lo}")
+            listed = offsets[:, lo * K // PER_COLUMN : hi * K // PER_COLUMN]
+            nc.vector.tensor_tensor(products[:], planes[t][:].indirect(listed), weights_flat[:, lo * K : hi * K], MULT)
+            return products
+
+        def add_corners(t, lo, hi, products):
+            with nc.allow_low_precision(reason="float32 sum, rounded once to bfloat16 on the way out"):
+                nc.vector.tensor_reduce(
+                    out=e_grouped[:, lo:hi, t],
+                    in_=products[:].rearrange("p (g j) -> p g j", j=K),
+                    axis=mybir.AxisListType.X,
+                    op=ADD,
+                )
+
+        def quantize(grouped, codes, scales, lo, hi):
+            nc.vector.quantize_mx(
+                out=codes[:, lo:hi].bitcast(FP8X4),
+                scales=scales[:, lo:hi],
+                in_=grouped[:, lo:hi, :].rearrange("p c t -> p (c t)"),
+            )
+
+        def group_w(c):
+            run = [i for i, (lo, hi) in enumerate(W_RUNS) if lo <= c * P < hi][0]
+            first = c * P - W_RUNS[run][0]
+            nc.scalar.copy(
+                out=w_grouped[:, c * P : (c + 1) * P, :].rearrange("p (c i) t -> p c t i", i=4),
+                in_=w_raw[run][:, :, first : first + P].rearrange("p t (c i) -> p c t i", i=4),
+            )
+
+        for t in range(PACK - 1):
+            add_corners(t, 0, G, gather(t, 0, G))
+
+        last = PACK - 1
+        for c in range(M_TILES):
+            group_w(c)
+        (a0, a1), (b0, b1) = POINT_RUNS
+        products_a = gather(last, a0, a1)
+        products_b = gather(last, b0, b1)
+        add_corners(last, a0, a1, products_a)
+        quantize(w_grouped, w_codes, w_scales, *W_RUNS[0])
+        quantize(e_grouped, e_codes, e_scales, a0, a1)
+        add_corners(last, b0, b1, products_b)
+        quantize(w_grouped, w_codes, w_scales, *W_RUNS[1])
+        quantize(e_grouped, e_codes, e_scales, b0, b1)
+
+        out_rows = out.rearrange("(c p) g -> p c g", p=P)
+        for lo, hi in POINT_RUNS:
+            result = keep.tile([P, M_TILES, hi - lo], F32, name=f"result{lo}")
+            for c in range(M_TILES):
+                acc = psum.tile([P, hi - lo], F32, name=f"acc{lo}_{c}")
+                nc.tensor.matmul_mx(
+                    out=acc[:],
+                    lhsT=w_codes[:, c * P : (c + 1) * P].bitcast(FP8X4),
+                    lhsT_scale=w_scales[:, c * P : (c + 1) * P],
+                    rhs=e_codes[:, lo:hi].bitcast(FP8X4),
+                    rhs_scale=e_scales[:, lo:hi],
+                    start=True,
+                    stop=True,
+                )
+                if hi == G and c != 1:
+                    nc.vector.tensor_scalar(result[:, c, :], acc[:], bias_cols[:, c : c + 1], None, ADD)
+                else:
+                    nc.scalar.activation(result[:, c, :], acc[:], IDENTITY, bias=bias_cols[:, c : c + 1])
+            nc.sync.dma_start(out=out_rows[:, :, lo:hi], in_=result[:])

@@ -109,7 +109,8 @@ def tile_attend_grid_bias_kernel(tc, xT, w, part, bias, offs, out):
         products_a = gather(last, a0, a1)
         products_b = gather(last, b0, b1)
         add_corners(last, a0, a1, products_a)
-        quantize(w_grouped, w_codes, w_scales, *W_RUNS[0])
+        quantize(w_grouped, w_codes, w_scales, 0, P)
+        quantize(w_grouped, w_codes, w_scales, P, 2 * P)
         quantize(e_grouped, e_codes, e_scales, a0, a1)
         add_corners(last, b0, b1, products_b)
         quantize(w_grouped, w_codes, w_scales, *W_RUNS[1])
@@ -133,4 +134,7 @@ def tile_attend_grid_bias_kernel(tc, xT, w, part, bias, offs, out):
                     nc.vector.tensor_scalar(result[:, c, :], acc[:], bias_cols[:, c : c + 1], None, ADD)
                 else:
                     nc.scalar.activation(result[:, c, :], acc[:], IDENTITY, bias=bias_cols[:, c : c + 1])
-            nc.sync.dma_start(out=out_rows[:, :, lo:hi], in_=result[:])
+                if hi == G:
+                    nc.sync.dma_start(out=out_rows[:, c, lo:hi], in_=result[:, c, :])
+            if hi < G:
+                nc.sync.dma_start(out=out_rows[:, :, lo:hi], in_=result[:])

from contextlib import ExitStack

import concourse.mybir as mybir
from concourse.masks import make_identity

G, K, T, D, M = 256, 4, 4096, 512, 384
FLOPS = 2 * D * M * G
BYTES = 4 * (D * T + D * M + G * K + M + M * G) + 2 * 128 * (G * K // 16)

F32 = mybir.dt.float32
BF16 = mybir.dt.bfloat16
U32 = mybir.dt.uint32
U16 = mybir.dt.uint16
U8 = mybir.dt.uint8
FP8X4 = mybir.dt.float8_e4m3fn_x4
MULT = mybir.AluOpType.mult
ADD = mybir.AluOpType.add
IDENTITY = mybir.ActivationFunctionType.Identity

P = 128
PACK = 4
ENTRIES = G * K
PER_COLUMN = 16
M_TILES = M // P
PART_ROW = ENTRIES // P
POINT_RUNS = ((0, 128), (128, 256))
W_RUNS = ((0, 256), (256, 384))


def tile_attend_grid_bias_kernel(tc, xT, w, part, bias, offs, out):
    nc = tc.nc
    with ExitStack() as ctx:
        keep = ctx.enter_context(tc.tile_pool(name="keep", bufs=1))
        psum = ctx.enter_context(tc.psum_pool(name="psum", bufs=1))

        offsets = keep.tile([P, ENTRIES // PER_COLUMN], U16, name="offsets")
        part_rows = keep.tile([P, PART_ROW], F32, name="part_rows")
        planes = [keep.tile([P, T], F32, name=f"plane{t}") for t in range(PACK)]
        w_raw = [keep.tile([P, PACK, hi - lo], F32, name=f"w_raw{lo}") for lo, hi in W_RUNS]
        bias_cols = keep.tile([P, M_TILES], F32, name="bias_cols")

        x_rows = xT.rearrange("(p t) c -> p t c", t=PACK)
        w_rows = w.rearrange("(p t) m -> p t m", t=PACK)
        nc.scalar.dma_start(out=part_rows[:], in_=part[0:1, :].rearrange("o (n r) -> (o n) r", r=PART_ROW))
        nc.sync.dma_start(out=planes[0][:], in_=x_rows[:, 0, :])
        nc.sync.dma_start(offsets[:], offs)
        for t in range(1, PACK):
            nc.sync.dma_start(out=planes[t][:], in_=x_rows[:, t, :])
        for raw, (lo, hi) in zip(w_raw, W_RUNS):
            nc.sync.dma_start(out=raw[:], in_=w_rows[:, :, lo:hi])
        with nc.allow_non_contiguous_dma(reason="one bias value to a partition"):
            nc.sync.dma_start(out=bias_cols[:], in_=bias.rearrange("(c p) o -> p (c o)", p=P))

        identity = keep.tile([P, P], F32, name="identity")
        make_identity(nc, identity[:])
        weights = keep.tile([P, P, PART_ROW], F32, name="weights")
        for half in range(2):
            spread = psum.tile([P, 4, P], F32, name=f"spread{half}")
            for r in range(4):
                column = part_rows[:, 4 * half + r : 4 * half + r + 1]
                nc.tensor.transpose(spread[:, r, :], column.to_broadcast([P, P]), identity[:])
            nc.scalar.copy(out=weights[:, :, 4 * half : 4 * half + 4], in_=spread[:].rearrange("p r n -> p n r"))
        weights_flat = weights[:].rearrange("p n r -> p (n r)")

        e_grouped = keep.tile([P, G, PACK], BF16, name="e_grouped", align_bytes=64)
        e_codes = keep.tile([P, G], U32, name="e_codes", align_bytes=64)
        e_scales = keep.tile([P, G], U8, name="e_scales", align_bytes=64)
        w_grouped = keep.tile([P, M, PACK], BF16, name="w_grouped", align_bytes=64)
        w_codes = keep.tile([P, M], U32, name="w_codes", align_bytes=64)
        w_scales = keep.tile([P, M], U8, name="w_scales", align_bytes=64)

        def gather(t, lo, hi):
            products = keep.tile([P, (hi - lo) * K], F32, name=f"products{t}_{lo}")
            listed = offsets[:, lo * K // PER_COLUMN : hi * K // PER_COLUMN]
            nc.vector.tensor_tensor(products[:], planes[t][:].indirect(listed), weights_flat[:, lo * K : hi * K], MULT)
            return products

        def add_corners(t, lo, hi, products):
            with nc.allow_low_precision(reason="float32 sum, rounded once to bfloat16 on the way out"):
                nc.vector.tensor_reduce(
                    out=e_grouped[:, lo:hi, t],
                    in_=products[:].rearrange("p (g j) -> p g j", j=K),
                    axis=mybir.AxisListType.X,
                    op=ADD,
                )

        def quantize(grouped, codes, scales, lo, hi):
            nc.vector.quantize_mx(
                out=codes[:, lo:hi].bitcast(FP8X4),
                scales=scales[:, lo:hi],
                in_=grouped[:, lo:hi, :].rearrange("p c t -> p (c t)"),
            )

        def group_w(c):
            run = [i for i, (lo, hi) in enumerate(W_RUNS) if lo <= c * P < hi][0]
            first = c * P - W_RUNS[run][0]
            nc.scalar.copy(
                out=w_grouped[:, c * P : (c + 1) * P, :].rearrange("p (c i) t -> p c t i", i=4),
                in_=w_raw[run][:, :, first : first + P].rearrange("p t (c i) -> p c t i", i=4),
            )

        for t in range(PACK - 1):
            add_corners(t, 0, G, gather(t, 0, G))

        last = PACK - 1
        for c in range(M_TILES):
            group_w(c)
        (a0, a1), (b0, b1) = POINT_RUNS
        products_a = gather(last, a0, a1)
        products_b = gather(last, b0, b1)
        add_corners(last, a0, a1, products_a)
        quantize(w_grouped, w_codes, w_scales, 0, P)
        quantize(w_grouped, w_codes, w_scales, P, 2 * P)
        quantize(e_grouped, e_codes, e_scales, a0, a1)
        add_corners(last, b0, b1, products_b)
        quantize(w_grouped, w_codes, w_scales, *W_RUNS[1])
        quantize(e_grouped, e_codes, e_scales, b0, b1)

        out_rows = out.rearrange("(c p) g -> p c g", p=P)
        for lo, hi in POINT_RUNS:
            result = keep.tile([P, M_TILES, hi - lo], F32, name=f"result{lo}")
            for c in range(M_TILES):
                acc = psum.tile([P, hi - lo], F32, name=f"acc{lo}_{c}")
                nc.tensor.matmul_mx(
                    out=acc[:],
                    lhsT=w_codes[:, c * P : (c + 1) * P].bitcast(FP8X4),
                    lhsT_scale=w_scales[:, c * P : (c + 1) * P],
                    rhs=e_codes[:, lo:hi].bitcast(FP8X4),
                    rhs_scale=e_scales[:, lo:hi],
                    start=True,
                    stop=True,
                )
                if hi == G and c != 1:
                    nc.vector.tensor_scalar(result[:, c, :], acc[:], bias_cols[:, c : c + 1], None, ADD)
                else:
                    nc.scalar.activation(result[:, c, :], acc[:], IDENTITY, bias=bias_cols[:, c : c + 1])
                if hi == G:
                    nc.sync.dma_start(out=out_rows[:, c, lo:hi], in_=result[:, c, :])
            if hi < G:
                nc.sync.dma_start(out=out_rows[:, :, lo:hi], in_=result[:])
